import numpy as np
import ml_dtypes


def mxq(x, axis, fmt="e4m3"):
    dtype, down = {"e4m3": (ml_dtypes.float8_e4m3fn, 7), "e5m2": (ml_dtypes.float8_e5m2, 14)}[fmt]
    v = np.moveaxis(np.asarray(x, np.float32).astype(ml_dtypes.bfloat16).astype(np.float64), axis, -1)
    blocks = v.reshape(v.shape[:-1] + (-1, 32))
    amax = np.abs(blocks).max(-1, keepdims=True)
    byte = np.maximum(np.where(amax > 0, np.frexp(amax)[1] - 1 + 127, 0) - down, 1)
    scale = np.exp2(byte - 127.0)
    codes = (blocks / scale).astype(np.float32).astype(dtype).astype(np.float64)
    return np.moveaxis((codes * scale).reshape(v.shape), -1, axis)


WIDE = False


def mx_kscale(k):
    if not WIDE:
        return np.ones(k)
    levels = np.array([24, -24, 12, -12, 0])
    if k % 512:
        return np.exp2(np.random.permutation(np.resize(levels, k // 32))).repeat(32)
    a = np.empty((k // 512, 16))
    for p in range(k // 512):
        a[p, :8] = np.random.permutation(np.resize(levels, 8))
        for g in range(8):
            far = levels[np.abs(levels - a[p, g]) >= 10]
            a[p, g + 8] = far[np.random.randint(len(far))]
    return np.exp2(a.ravel()).repeat(32)


def f64(x):
    return np.asarray(x).astype(np.float64)


def striped8(idx):
    return np.concatenate([v.reshape(-1, 16).T for v in idx]).astype(np.uint16)


def unstriped8(offs):
    return np.stack([offs[16 * g:16 * g + 16].T.reshape(-1) for g in range(8)]).astype(np.int64)


K, L, N, T, J = 512, 512, 512, 2048, 1024


def setup_inputs():
    n = np.random.standard_normal
    s = mx_kscale(K)[:, None]
    s2 = mx_kscale(L)[:, None]
    return {
        "xT": (n((K, T)) * s).astype(np.float32),
        "wgt": np.repeat(np.random.uniform(0.5, 2.0, (8, J)), 16, axis=0).astype(np.float32),
        "zT": (n((L, T)) * s2).astype(np.float32),
        "wgt2": np.repeat(np.random.uniform(0.5, 2.0, (8, J)), 16, axis=0).astype(np.float32),
        "wa": (n((K, N)) / np.sqrt(K) / s).astype(np.float32),
        "wb": (n((L, N)) / np.sqrt(L) / s2).astype(np.float32),
        "b": (0.3 * n(N)).astype(np.float32),
        "offs": striped8(np.stack([np.random.permutation(T)[:J] for _ in range(8)])),
        "offs2": striped8(np.stack([np.random.permutation(T)[:J] for _ in range(8)])),
    }


def reference(xT, wgt, zT, wgt2, wa, wb, b, offs, offs2):
    idx = unstriped8(offs)
    idx2 = unstriped8(offs2)
    rows = np.arange(K)
    xg = f64(wgt)[rows // 4 % 128] * f64(xT)[rows[:, None], idx[rows % 512 // 64]]
    xT_ = mxq(xg, 0, "e4m3")
    rows = np.arange(L)
    xg = f64(wgt2)[rows // 4 % 128] * f64(zT)[rows[:, None], idx2[rows % 512 // 64]]
    zT_ = mxq(xg, 0, "e4m3")
    wa_ = mxq(f64(wa), 0, "e4m3")
    wb_ = mxq(f64(wb), 0, "e4m3")
    ya = wa_.T @ xT_
    yb = wb_.T @ zT_
    return np.maximum(ya, yb) + f64(b)[:, None]

@@ -1,0 +1,134 @@
+from contextlib import ExitStack
+
+import concourse.mybir as mybir
+
+K, N, T, J = 512, 512, 2048, 1024
+FLOPS = 2 * 2 * K * N * J
+
+F32 = mybir.dt.float32
+BF16 = mybir.dt.bfloat16
+U32 = mybir.dt.uint32
+U16 = mybir.dt.uint16
+U8 = mybir.dt.uint8
+FP8X4 = mybir.dt.float8_e4m3fn_x4
+ALU = mybir.AluOpType
+ACT = mybir.ActivationFunctionType
+
+P = 128
+PACK = 4
+N_TILES = N // P
+X_CHUNK = 512
+Z_CHUNK = 256
+
+
+def tile_list_max_bias_kernel(tc, xT, wgt, zT, wgt2, wa, wb, b, offs, offs2, out):
+    nc = tc.nc
+    with ExitStack() as ctx:
+        keep = ctx.enter_context(tc.tile_pool(name="keep", bufs=1))
+        psum = ctx.enter_context(tc.psum_pool(name="psum", bufs=8))
+
+        def load(name, shape, dtype, src):
+            t = keep.tile(shape, dtype, name=name, align_bytes=64)
+            nc.sync.dma_start(t[:], src)
+            return t
+
+        x_rows = xT.rearrange("(p t) s -> p t s", t=PACK)
+        z_rows = zT.rearrange("(p t) s -> p t s", t=PACK)
+        wb_rows = wb.rearrange("(p t) n -> p t n", t=PACK)
+
+        x_list = load("x_list", [P, J // 16], U16, offs)
+        x_wgt = [load("x_wgt0", [P, X_CHUNK], F32, wgt[:, 0:X_CHUNK])]
+        x_planes = [load("x_plane0", [P, T], F32, x_rows[:, 0, :])]
+        x_wgt.append(load("x_wgt1", [P, X_CHUNK], F32, wgt[:, X_CHUNK:J]))
+        for t in range(1, PACK):
+            x_planes.append(load("x_plane%d" % t, [P, T], F32, x_rows[:, t, :]))
+        z_list = load("z_list", [P, J // 16], U16, offs2)
+        z_wgt = load("z_wgt", [P, J], F32, wgt2)
+        z_planes = [load("z_plane0", [P, T], F32, z_rows[:, 0, :])]
+        wa_raw = load("wa_raw", [P, PACK, N], F32, wa.rearrange("(p t) n -> p t n", t=PACK))
+        with nc.allow_non_contiguous_dma(reason="bias, one value a partition"):
+            bias = load("bias", [P, N_TILES], F32, b.rearrange("(m p) -> p m", p=P))
+        for t in range(1, PACK):
+            z_planes.append(load("z_plane%d" % t, [P, T], F32, z_rows[:, t, :]))
+        wb_raw = [load("wb_raw%d" % h, [P, PACK, N // 2], F32, wb_rows[:, :, h * N // 2 : (h + 1) * N // 2]) for h in range(2)]
+
+        def gather(dst, plane, lst, weights, j0, width):
+            nc.vector.tensor_tensor(
+                dst, plane[:].indirect(lst[:, j0 // 16 : (j0 + width) // 16]), weights, ALU.mult
+            )
+
+        def weave(name, src, width):
+            woven = keep.tile([P, width, PACK], BF16, name=name + "_woven", align_bytes=64)
+            nc.scalar.copy(
+                woven[:].rearrange("p (c i) t -> p c t i", i=4),
+                src[:].rearrange("p t (c i) -> p c t i", i=4),
+            )
+            return woven
+
+        def quantise(name, woven, width):
+            codes = keep.tile([P, width], U32, name=name + "_codes", align_bytes=64)
+            scales = keep.tile([P, width], U8, name=name + "_scales", align_bytes=64)
+            nc.vector.quantize_mx(
+                out=codes[:].bitcast(FP8X4), scales=scales[:], in_=woven[:].rearrange("p w t -> p (w t)")
+            )
+            return codes, scales
+
+        def product(w_q, col, a_q, width):
+            acc = psum.tile([P, 512], F32, name="acc")
+            nc.tensor.matmul_mx(
+                out=acc[:, 0:width],
+                lhsT=w_q[0][:, col : col + P].bitcast(FP8X4),
+                lhsT_scale=w_q[1][:, col : col + P],
+                rhs=a_q[0][:].bitcast(FP8X4),
+                rhs_scale=a_q[1][:],
+                start=True,
+                stop=True,
+            )
+            return acc
+
+        x_chunks = range(J // X_CHUNK)
+        xg = [keep.tile([P, PACK, X_CHUNK], F32, name="xg%d" % c) for c in x_chunks]
+        for t in range(PACK):
+            for c in x_chunks:
+                gather(xg[c][:, t, :], x_planes[t], x_list, x_wgt[c][:], c * X_CHUNK, X_CHUNK)
+        z_chunks = range(J // Z_CHUNK)
+        zg = [keep.tile([P, PACK, Z_CHUNK], F32, name="zg%d" % c) for c in z_chunks]
+        for t in range(PACK):
+            for c in z_chunks:
+                j0 = c * Z_CHUNK
+                gather(zg[c][:, t, :], z_planes[t], z_list, z_wgt[:, j0 : j0 + Z_CHUNK], j0, Z_CHUNK)
+
+        x_woven = [weave("x%d" % c, xg[c], X_CHUNK) for c in x_chunks]
+        wa_woven = weave("wa", wa_raw, N)
+        x_q = [quantise("x%d" % c, x_woven[c], X_CHUNK) for c in x_chunks]
+        wa_q = quantise("wa", wa_woven, N)
+        ya = []
+        for c in x_chunks:
+            ya_c = keep.tile([P, N_TILES, X_CHUNK], F32, name="ya%d" % c)
+            for m in range(N_TILES):
+                acc = product(wa_q, m * P, x_q[c], X_CHUNK)
+                nc.scalar.activation(ya_c[:, m, :], acc[:], ACT.Identity, bias=bias[:, m : m + 1])
+            ya.append(ya_c)
+
+        z_q, wb_q = [], []
+        for c in z_chunks:
+            z_q.append(quantise("z%d" % c, weave("z%d" % c, zg[c], Z_CHUNK), Z_CHUNK))
+            if c < 2:
+                wb_q.append(quantise("wb%d" % c, weave("wb%d" % c, wb_raw[c], N // 2), N // 2))
+        out_rows = out.rearrange("(m p) j -> p m j", p=P)
+        for c, half in ((0, 0), (1, 0), (0, 1), (1, 1), (2, 0), (2, 1), (3, 0), (3, 1)):
+            j0 = c * Z_CHUNK
+            jj = j0 % X_CHUNK
+            res = keep.tile([P, 2, Z_CHUNK], F32, name="res%d_%d" % (c, half))
+            for mm in range(2):
+                m = 2 * half + mm
+                acc = product(wb_q[half], mm * P, z_q[c], Z_CHUNK)
+                nc.vector.scalar_tensor_tensor(
+                    out=res[:, mm, :],
+                    in0=acc[:, 0:Z_CHUNK],
+                    scalar=bias[:, m : m + 1],
+                    in1=ya[j0 // X_CHUNK][:, m, jj : jj + Z_CHUNK],
+                    op0=ALU.add,
+                    op1=ALU.max,
+                )
+            nc.sync.dma_start(out_rows[:, 2 * half : 2 * half + 2, j0 : j0 + Z_CHUNK], res[:])

@@ -1,6 +1,7 @@
 from contextlib import ExitStack
 
 import concourse.mybir as mybir
+from concourse.masks import make_identity
 
 K, N, T, J = 512, 512, 2048, 1024
 FLOPS = 2 * 2 * K * N * J
@@ -17,8 +18,9 @@ ACT = mybir.ActivationFunctionType
 P = 128
 PACK = 4
 N_TILES = N // P
-X_CHUNK = 512
-Z_CHUNK = 256
+CHUNK = 256
+HALF = N // 2
+WIDE = 512
 
 
 def tile_list_max_bias_kernel(tc, xT, wgt, zT, wgt2, wa, wb, b, offs, offs2, out):
@@ -28,7 +30,7 @@ def tile_list_max_bias_kernel(tc, xT, wgt, zT, wgt2, wa, wb, b, offs, offs2, out
         psum = ctx.enter_context(tc.psum_pool(name="psum", bufs=8))
 
         def load(name, shape, dtype, src):
-            t = keep.tile(shape, dtype, name=name, align_bytes=64)
+            t = keep.tile(shape, dtype, name=name, tag=name, align_bytes=64)
             nc.sync.dma_start(t[:], src)
             return t
 
@@ -37,36 +39,46 @@ def tile_list_max_bias_kernel(tc, xT, wgt, zT, wgt2, wa, wb, b, offs, offs2, out
         wb_rows = wb.rearrange("(p t) n -> p t n", t=PACK)
 
         x_list = load("x_list", [P, J // 16], U16, offs)
-        x_wgt = [load("x_wgt0", [P, X_CHUNK], F32, wgt[:, 0:X_CHUNK])]
+        x_wgt = keep.tile([P, J], F32, name="x_wgt")
+        nc.sync.dma_start(x_wgt[:, 0:CHUNK], wgt[:, 0:CHUNK])
         x_planes = [load("x_plane0", [P, T], F32, x_rows[:, 0, :])]
-        x_wgt.append(load("x_wgt1", [P, X_CHUNK], F32, wgt[:, X_CHUNK:J]))
+        nc.sync.dma_start(x_wgt[:, CHUNK:J], wgt[:, CHUNK:J])
         for t in range(1, PACK):
             x_planes.append(load("x_plane%d" % t, [P, T], F32, x_rows[:, t, :]))
+        wa_raw = load("wa_raw", [P, PACK, N], F32, wa.rearrange("(p t) n -> p t n", t=PACK))
         z_list = load("z_list", [P, J // 16], U16, offs2)
         z_wgt = load("z_wgt", [P, J], F32, wgt2)
         z_planes = [load("z_plane0", [P, T], F32, z_rows[:, 0, :])]
-        wa_raw = load("wa_raw", [P, PACK, N], F32, wa.rearrange("(p t) n -> p t n", t=PACK))
-        with nc.allow_non_contiguous_dma(reason="bias, one value a partition"):
-            bias = load("bias", [P, N_TILES], F32, b.rearrange("(m p) -> p m", p=P))
-        for t in range(1, PACK):
+        for t in range(1, PACK - 1):
             z_planes.append(load("z_plane%d" % t, [P, T], F32, z_rows[:, t, :]))
-        wb_raw = [load("wb_raw%d" % h, [P, PACK, N // 2], F32, wb_rows[:, :, h * N // 2 : (h + 1) * N // 2]) for h in range(2)]
+        wb_raw = [load("wb_raw0", [P, PACK, HALF], F32, wb_rows[:, :, 0:HALF])]
+        z_planes.append(load("z_plane3", [P, T], F32, z_rows[:, PACK - 1, :]))
+        wb_raw.append(load("wb_raw1", [P, PACK, HALF], F32, wb_rows[:, :, HALF:N]))
 
-        def gather(dst, plane, lst, weights, j0, width):
-            nc.vector.tensor_tensor(
-                dst, plane[:].indirect(lst[:, j0 // 16 : (j0 + width) // 16]), weights, ALU.mult
-            )
+        ident = keep.tile([P, P], F32, name="ident")
+        make_identity(nc, ident[:])
+        b_rows = keep.tile([P, P], F32, name="b_rows")
+        nc.gpsimd.memset(b_rows[:], 0.0)
+        nc.scalar.dma_start(b_rows[0:N_TILES, :], b.rearrange("(m p) -> m p", p=P))
+        b_turned = psum.tile([P, 512], F32, name="acc")
+        nc.tensor.transpose(b_turned[:, 0:P], b_rows[:], ident[:])
+        bias = keep.tile([P, N_TILES], F32, name="bias")
+        nc.scalar.copy(bias[:], b_turned[:, 0:N_TILES])
 
-        def weave(name, src, width):
-            woven = keep.tile([P, width, PACK], BF16, name=name + "_woven", align_bytes=64)
-            nc.scalar.copy(
-                woven[:].rearrange("p (c i) t -> p c t i", i=4),
-                src[:].rearrange("p t (c i) -> p c t i", i=4),
-            )
-            return woven
+        def gather(dst, planes, t, lst, weights, cuts):
+            for j0, j1 in zip(cuts[:-1], cuts[1:]):
+                nc.vector.tensor_tensor(
+                    dst[:, t, j0:j1], planes[t][:].indirect(lst[:, j0 // 16 : j1 // 16]), weights[:, j0:j1], ALU.mult
+                )
 
-        def quantise(name, woven, width):
-            codes = keep.tile([P, width], U32, name=name + "_codes", align_bytes=64)
+        def weave(copy, dst, src):
+            copy(dst.rearrange("p (c i) t -> p c t i", i=4), src.rearrange("p t (c i) -> p c t i", i=4))
+
+        def woven_tile(name, width):
+            return keep.tile([P, width, PACK], BF16, name=name, tag=name, align_bytes=64)
+
+        def quantise(name, woven, width, behind=None):
+            codes = keep.tile([P, width], U32, name=name + "_codes", tag=behind or name + "_codes", align_bytes=64)
             scales = keep.tile([P, width], U8, name=name + "_scales", align_bytes=64)
             nc.vector.quantize_mx(
                 out=codes[:].bitcast(FP8X4), scales=scales[:], in_=woven[:].rearrange("p w t -> p (w t)")
@@ -86,49 +98,51 @@ def tile_list_max_bias_kernel(tc, xT, wgt, zT, wgt2, wa, wb, b, offs, offs2, out
             )
             return acc
 
-        x_chunks = range(J // X_CHUNK)
-        xg = [keep.tile([P, PACK, X_CHUNK], F32, name="xg%d" % c) for c in x_chunks]
-        for t in range(PACK):
-            for c in x_chunks:
-                gather(xg[c][:, t, :], x_planes[t], x_list, x_wgt[c][:], c * X_CHUNK, X_CHUNK)
-        z_chunks = range(J // Z_CHUNK)
-        zg = [keep.tile([P, PACK, Z_CHUNK], F32, name="zg%d" % c) for c in z_chunks]
-        for t in range(PACK):
-            for c in z_chunks:
-                j0 = c * Z_CHUNK
-                gather(zg[c][:, t, :], z_planes[t], z_list, z_wgt[:, j0 : j0 + Z_CHUNK], j0, Z_CHUNK)
+        whole = (0, J)
+        early = (0, CHUNK, J)
+        late = (0, CHUNK, WIDE, J)
+        xg = keep.tile([P, PACK, J], F32, name="xg")
+        zg = keep.tile([P, PACK, J], F32, name="zg")
+        for t, cuts in enumerate((early, whole, whole, late)):
+            gather(xg, x_planes, t, x_list, x_wgt, cuts)
+        for t, cuts in enumerate((whole, whole, whole, late)):
+            gather(zg, z_planes, t, z_list, z_wgt, cuts)
 
-        x_woven = [weave("x%d" % c, xg[c], X_CHUNK) for c in x_chunks]
-        wa_woven = weave("wa", wa_raw, N)
-        x_q = [quantise("x%d" % c, x_woven[c], X_CHUNK) for c in x_chunks]
+        x_woven = [woven_tile("x_woven%d" % h, WIDE) for h in range(2)]
+        for h in range(2):
+            weave(nc.scalar.copy, x_woven[h][:, :, 0:2], xg[:, 0:2, h * WIDE : (h + 1) * WIDE])
+        for j0, j1 in zip(late[:-1], late[1:]):
+            h = j0 // WIDE
+            weave(nc.scalar.copy, x_woven[h][:, j0 - h * WIDE : j1 - h * WIDE, 2:4], xg[:, 2:4, j0:j1])
+        x_q = [quantise("x%d" % h, x_woven[h], WIDE) for h in range(2)]
+        wa_woven = woven_tile("wa_woven", N)
+        weave(nc.vector.tensor_copy, wa_woven[:], wa_raw[:])
         wa_q = quantise("wa", wa_woven, N)
-        ya = []
-        for c in x_chunks:
-            ya_c = keep.tile([P, N_TILES, X_CHUNK], F32, name="ya%d" % c)
+        ya = [keep.tile([P, J], F32, name="ya%d" % m) for m in range(N_TILES)]
+        for h in range(2):
             for m in range(N_TILES):
-                acc = product(wa_q, m * P, x_q[c], X_CHUNK)
-                nc.scalar.activation(ya_c[:, m, :], acc[:], ACT.Identity, bias=bias[:, m : m + 1])
-            ya.append(ya_c)
+                acc = product(wa_q, m * P, x_q[h], WIDE)
+                nc.scalar.activation(ya[m][:, h * WIDE : (h + 1) * WIDE], acc[:], ACT.Identity, bias=bias[:, m : m + 1])
 
-        z_q, wb_q = [], []
-        for c in z_chunks:
-            z_q.append(quantise("z%d" % c, weave("z%d" % c, zg[c], Z_CHUNK), Z_CHUNK))
-            if c < 2:
-                wb_q.append(quantise("wb%d" % c, weave("wb%d" % c, wb_raw[c], N // 2), N // 2))
-        out_rows = out.rearrange("(m p) j -> p m j", p=P)
-        for c, half in ((0, 0), (1, 0), (0, 1), (1, 1), (2, 0), (2, 1), (3, 0), (3, 1)):
-            j0 = c * Z_CHUNK
-            jj = j0 % X_CHUNK
-            res = keep.tile([P, 2, Z_CHUNK], F32, name="res%d_%d" % (c, half))
-            for mm in range(2):
-                m = 2 * half + mm
-                acc = product(wb_q[half], mm * P, z_q[c], Z_CHUNK)
+        z_woven = [woven_tile("z_woven%d" % h, WIDE) for h in range(2)]
+        wb_woven = [woven_tile("wb_woven%d" % h, HALF) for h in range(2)]
+        weave(nc.scalar.copy, wb_woven[0][:], wb_raw[0][:])
+        for j0 in (0, CHUNK):
+            weave(nc.scalar.copy, z_woven[0][:, j0 : j0 + CHUNK, :], zg[:, :, j0 : j0 + CHUNK])
+        weave(nc.scalar.copy, wb_woven[1][:], wb_raw[1][:])
+        weave(nc.scalar.copy, z_woven[1][:], zg[:, :, WIDE:J])
+        wb_q = [quantise("wb0", wb_woven[0], HALF, "z_wgt")]
+        z_q = [quantise("z0", z_woven[0], WIDE)]
+        wb_q.append(quantise("wb1", wb_woven[1], HALF))
+        z_q.append(quantise("z1", z_woven[1], WIDE))
+        for h in range(2):
+            cols = slice(h * WIDE, (h + 1) * WIDE)
+            for m in range(N_TILES):
+                name = "res%d_%d" % (h, m)
+                tag = "z_woven1" if (h, m) == (0, N_TILES - 1) else name
+                res = keep.tile([P, WIDE], F32, name=name, tag=tag, align_bytes=64)
+                acc = product(wb_q[m // 2], m % 2 * P, z_q[h], WIDE)
                 nc.vector.scalar_tensor_tensor(
-                    out=res[:, mm, :],
-                    in0=acc[:, 0:Z_CHUNK],
-                    scalar=bias[:, m : m + 1],
-                    in1=ya[j0 // X_CHUNK][:, m, jj : jj + Z_CHUNK],
-                    op0=ALU.add,
-                    op1=ALU.max,
+                    out=res[:], in0=acc[:], scalar=bias[:, m : m + 1], in1=ya[m][:, cols], op0=ALU.add, op1=ALU.max
                 )
-            nc.sync.dma_start(out_rows[:, 2 * half : 2 * half + 2, j0 : j0 + Z_CHUNK], res[:])
+                nc.sync.dma_start(out[m * P : (m + 1) * P, cols], res[:])

@@ -17,10 +17,15 @@ ACT = mybir.ActivationFunctionType
 
 P = 128
 PACK = 4
+HEADS = 8
+HEAD_ROWS = P // HEADS
+BANK = 512
 N_TILES = N // P
-CHUNK = 256
+J_BLOCKS = J // P
+WIDE = BANK
+CHUNK = WIDE // 2
 HALF = N // 2
-WIDE = 512
+HELD_TILE = 2
 
 
 def tile_list_max_bias_kernel(tc, xT, wgt, zT, wgt2, wa, wb, b, offs, offs2, out):
@@ -30,46 +35,62 @@ def tile_list_max_bias_kernel(tc, xT, wgt, zT, wgt2, wa, wb, b, offs, offs2, out
         psum = ctx.enter_context(tc.psum_pool(name="psum", bufs=8))
 
         def load(name, shape, dtype, src):
-            t = keep.tile(shape, dtype, name=name, tag=name, align_bytes=64)
-            nc.sync.dma_start(t[:], src)
-            return t
+            tile = keep.tile(shape, dtype, name=name, tag=name, align_bytes=64)
+            nc.sync.dma_start(tile[:], src)
+            return tile
 
         x_rows = xT.rearrange("(p t) s -> p t s", t=PACK)
         z_rows = zT.rearrange("(p t) s -> p t s", t=PACK)
-        wb_rows = wb.rearrange("(p t) n -> p t n", t=PACK)
-
-        x_list = load("x_list", [P, J // 16], U16, offs)
+        head_rows = keep.tile([P, P], F32, name="head_rows")
+        for s, w in enumerate((wgt, wgt2)):
+            rows = w.rearrange("(g r) (c i) -> r g c i", r=HEAD_ROWS, i=P)[0]
+            nc.sync.dma_start(head_rows[P // 2 * s : P // 2 * (s + 1), :], rows)
         x_wgt = keep.tile([P, J], F32, name="x_wgt")
+        z_wgt = [keep.tile([P, WIDE], F32, name="z_wgt%d" % h, tag="z_wgt%d" % h, align_bytes=64) for h in range(2)]
         nc.sync.dma_start(x_wgt[:, 0:CHUNK], wgt[:, 0:CHUNK])
-        x_planes = [load("x_plane0", [P, T], F32, x_rows[:, 0, :])]
-        nc.sync.dma_start(x_wgt[:, CHUNK:J], wgt[:, CHUNK:J])
-        for t in range(1, PACK):
-            x_planes.append(load("x_plane%d" % t, [P, T], F32, x_rows[:, t, :]))
+
+        x_list = load("x_list", [P, J // HEAD_ROWS], U16, offs)
+        x_planes = [load("x_plane%d" % t, [P, T], F32, x_rows[:, t, :]) for t in range(PACK)]
         wa_raw = load("wa_raw", [P, PACK, N], F32, wa.rearrange("(p t) n -> p t n", t=PACK))
-        z_list = load("z_list", [P, J // 16], U16, offs2)
-        z_wgt = load("z_wgt", [P, J], F32, wgt2)
-        z_planes = [load("z_plane0", [P, T], F32, z_rows[:, 0, :])]
-        for t in range(1, PACK - 1):
-            z_planes.append(load("z_plane%d" % t, [P, T], F32, z_rows[:, t, :]))
-        wb_raw = [load("wb_raw0", [P, PACK, HALF], F32, wb_rows[:, :, 0:HALF])]
+        z_list = load("z_list", [P, J // HEAD_ROWS], U16, offs2)
+        z_planes = [load("z_plane%d" % t, [P, T], F32, z_rows[:, t, :]) for t in range(PACK - 1)]
+        wb_raw = load("wb_raw", [P, PACK, N], F32, wb.rearrange("(p t) n -> p t n", t=PACK))
         z_planes.append(load("z_plane3", [P, T], F32, z_rows[:, PACK - 1, :]))
-        wb_raw.append(load("wb_raw1", [P, PACK, HALF], F32, wb_rows[:, :, HALF:N]))
 
         ident = keep.tile([P, P], F32, name="ident")
         make_identity(nc, ident[:])
         b_rows = keep.tile([P, P], F32, name="b_rows")
         nc.gpsimd.memset(b_rows[:], 0.0)
         nc.scalar.dma_start(b_rows[0:N_TILES, :], b.rearrange("(m p) -> m p", p=P))
-        b_turned = psum.tile([P, 512], F32, name="acc")
+
+        turned = psum.tile([P, BANK], F32, name="acc")
+        nc.tensor.transpose(turned[:, 0:P], head_rows[:], ident[:])
+        by_block = turned[:, 0:P].rearrange("i (s g c) -> i s c g", s=2, g=HEADS)
+
+        def spread(s, dst, c0, c1):
+            blocks = c1 - c0
+            wide = keep.tile([P, blocks, HEADS, HEAD_ROWS], F32, name="wide%d_%d" % (s, c0))
+            nc.scalar.copy(wide[:], by_block[:, s, c0:c1, :].unsqueeze(3).to_broadcast([P, blocks, HEADS, HEAD_ROWS]))
+            bank = psum.tile([P, BANK], F32, name="acc")
+            for c in range(blocks):
+                nc.tensor.transpose(
+                    bank[:, c * P : (c + 1) * P], wide[:, c, :, :].rearrange("i g r -> i (g r)"), ident[:]
+                )
+            nc.scalar.copy(dst, bank[:, 0 : blocks * P])
+
+        for j0, j1 in ((CHUNK, CHUNK + BANK), (CHUNK + BANK, J)):
+            spread(0, x_wgt[:, j0:j1], j0 // P, j1 // P)
+        for h in range(2):
+            spread(1, z_wgt[h][:], h * J_BLOCKS // 2, (h + 1) * J_BLOCKS // 2)
+
+        b_turned = psum.tile([P, BANK], F32, name="acc")
         nc.tensor.transpose(b_turned[:, 0:P], b_rows[:], ident[:])
         bias = keep.tile([P, N_TILES], F32, name="bias")
         nc.scalar.copy(bias[:], b_turned[:, 0:N_TILES])
 
-        def gather(dst, planes, t, lst, weights, cuts):
-            for j0, j1 in zip(cuts[:-1], cuts[1:]):
-                nc.vector.tensor_tensor(
-                    dst[:, t, j0:j1], planes[t][:].indirect(lst[:, j0 // 16 : j1 // 16]), weights[:, j0:j1], ALU.mult
-                )
+        def gather(dst, plane, offsets, weights, j0, j1):
+            picked = plane[:].indirect(offsets[:, j0 // HEAD_ROWS : j1 // HEAD_ROWS])
+            nc.vector.tensor_tensor(dst, picked, weights, ALU.mult)
 
         def weave(copy, dst, src):
             copy(dst.rearrange("p (c i) t -> p c t i", i=4), src.rearrange("p t (c i) -> p c t i", i=4))
@@ -77,18 +98,19 @@ def tile_list_max_bias_kernel(tc, xT, wgt, zT, wgt2, wa, wb, b, offs, offs2, out
         def woven_tile(name, width):
             return keep.tile([P, width, PACK], BF16, name=name, tag=name, align_bytes=64)
 
-        def quantise(name, woven, width, behind=None):
-            codes = keep.tile([P, width], U32, name=name + "_codes", tag=behind or name + "_codes", align_bytes=64)
+        def quantise(name, woven, tag):
+            width = woven.shape[1]
+            codes = keep.tile([P, width], U32, name=name + "_codes", tag=tag, align_bytes=64)
             scales = keep.tile([P, width], U8, name=name + "_scales", align_bytes=64)
             nc.vector.quantize_mx(
-                out=codes[:].bitcast(FP8X4), scales=scales[:], in_=woven[:].rearrange("p w t -> p (w t)")
+                out=codes[:].bitcast(FP8X4), scales=scales[:], in_=woven.rearrange("p w t -> p (w t)")
             )
             return codes, scales
 
-        def product(w_q, col, a_q, width):
-            acc = psum.tile([P, 512], F32, name="acc")
+        def product(w_q, col, a_q):
+            acc = psum.tile([P, BANK], F32, name="acc")
             nc.tensor.matmul_mx(
-                out=acc[:, 0:width],
+                out=acc[:],
                 lhsT=w_q[0][:, col : col + P].bitcast(FP8X4),
                 lhsT_scale=w_q[1][:, col : col + P],
                 rhs=a_q[0][:].bitcast(FP8X4),
@@ -99,49 +121,56 @@ def tile_list_max_bias_kernel(tc, xT, wgt, zT, wgt2, wa, wb, b, offs, offs2, out
             return acc
 
         whole = (0, J)
-        early = (0, CHUNK, J)
+        halves = (0, WIDE, J)
+        early = (0, CHUNK, CHUNK + BANK, J)
         late = (0, CHUNK, WIDE, J)
         xg = keep.tile([P, PACK, J], F32, name="xg")
-        zg = keep.tile([P, PACK, J], F32, name="zg")
+        zg = [keep.tile([P, PACK, WIDE], F32, name="zg%d" % h, tag="zg%d" % h, align_bytes=64) for h in range(2)]
         for t, cuts in enumerate((early, whole, whole, late)):
-            gather(xg, x_planes, t, x_list, x_wgt, cuts)
-        for t, cuts in enumerate((whole, whole, whole, late)):
-            gather(zg, z_planes, t, z_list, z_wgt, cuts)
+            for j0, j1 in zip(cuts[:-1], cuts[1:]):
+                gather(xg[:, t, j0:j1], x_planes[t], x_list, x_wgt[:, j0:j1], j0, j1)
+        for t, cuts in enumerate((halves, halves, halves, late)):
+            for j0, j1 in zip(cuts[:-1], cuts[1:]):
+                h = j0 // WIDE
+                part = slice(j0 - h * WIDE, j1 - h * WIDE)
+                gather(zg[h][:, t, part], z_planes[t], z_list, z_wgt[h][:, part], j0, j1)
 
         x_woven = [woven_tile("x_woven%d" % h, WIDE) for h in range(2)]
         for h in range(2):
             weave(nc.scalar.copy, x_woven[h][:, :, 0:2], xg[:, 0:2, h * WIDE : (h + 1) * WIDE])
-        for j0, j1 in zip(late[:-1], late[1:]):
-            h = j0 // WIDE
-            weave(nc.scalar.copy, x_woven[h][:, j0 - h * WIDE : j1 - h * WIDE, 2:4], xg[:, 2:4, j0:j1])
-        x_q = [quantise("x%d" % h, x_woven[h], WIDE) for h in range(2)]
+        for j0 in (0, CHUNK):
+            weave(nc.scalar.copy, x_woven[0][:, j0 : j0 + CHUNK, 2:4], xg[:, 2:4, j0 : j0 + CHUNK])
         wa_woven = woven_tile("wa_woven", N)
-        weave(nc.vector.tensor_copy, wa_woven[:], wa_raw[:])
-        wa_q = quantise("wa", wa_woven, N)
+        weave(nc.vector.tensor_copy, wa_woven[:, 0:HALF, :], wa_raw[:, :, 0:HALF])
+        weave(nc.scalar.copy, wa_woven[:, HALF:N, :], wa_raw[:, :, HALF:N])
+        weave(nc.scalar.copy, x_woven[1][:, :, 2:4], xg[:, 2:4, WIDE:J])
+        x_q = [quantise("x%d" % h, x_woven[h][:], "x%d_codes" % h) for h in range(2)]
+        wa_q = quantise("wa", wa_woven[:], "wa_codes")
         ya = [keep.tile([P, J], F32, name="ya%d" % m) for m in range(N_TILES)]
         for h in range(2):
             for m in range(N_TILES):
-                acc = product(wa_q, m * P, x_q[h], WIDE)
+                acc = product(wa_q, m * P, x_q[h])
                 nc.scalar.activation(ya[m][:, h * WIDE : (h + 1) * WIDE], acc[:], ACT.Identity, bias=bias[:, m : m + 1])
 
         z_woven = [woven_tile("z_woven%d" % h, WIDE) for h in range(2)]
-        wb_woven = [woven_tile("wb_woven%d" % h, HALF) for h in range(2)]
-        weave(nc.scalar.copy, wb_woven[0][:], wb_raw[0][:])
-        for j0 in (0, CHUNK):
-            weave(nc.scalar.copy, z_woven[0][:, j0 : j0 + CHUNK, :], zg[:, :, j0 : j0 + CHUNK])
-        weave(nc.scalar.copy, wb_woven[1][:], wb_raw[1][:])
-        weave(nc.scalar.copy, z_woven[1][:], zg[:, :, WIDE:J])
-        wb_q = [quantise("wb0", wb_woven[0], HALF, "z_wgt")]
-        z_q = [quantise("z0", z_woven[0], WIDE)]
-        wb_q.append(quantise("wb1", wb_woven[1], HALF))
-        z_q.append(quantise("z1", z_woven[1], WIDE))
+        wb_woven = woven_tile("wb_woven", N)
+        weave(nc.scalar.copy, wb_woven[:], wb_raw[:])
+        for j0, j1 in zip(late[:-1], late[1:]):
+            h = j0 // WIDE
+            part = slice(j0 - h * WIDE, j1 - h * WIDE)
+            weave(nc.scalar.copy, z_woven[h][:, part, :], zg[h][:, :, part])
+        wb_q = [quantise("wb0", wb_woven[:, 0:HALF, :], "z_wgt0")]
+        z_q = [quantise("z0", z_woven[0][:], "z0_codes")]
+        wb_q.append(quantise("wb1", wb_woven[:, HALF:N, :], "zg0"))
+        z_q.append(quantise("z1", z_woven[1][:], "z1_codes"))
+
         for h in range(2):
             cols = slice(h * WIDE, (h + 1) * WIDE)
             for m in range(N_TILES):
                 name = "res%d_%d" % (h, m)
-                tag = "z_woven1" if (h, m) == (0, N_TILES - 1) else name
+                tag = "zg1" if (h, m) == (0, HELD_TILE) else name
                 res = keep.tile([P, WIDE], F32, name=name, tag=tag, align_bytes=64)
-                acc = product(wb_q[m // 2], m % 2 * P, z_q[h], WIDE)
+                acc = product(wb_q[m * P // HALF], m * P % HALF, z_q[h])
                 nc.vector.scalar_tensor_tensor(
                     out=res[:], in0=acc[:], scalar=bias[:, m : m + 1], in1=ya[m][:, cols], op0=ALU.add, op1=ALU.max
                 )

from contextlib import ExitStack

import concourse.mybir as mybir
from concourse.masks import make_identity

K, N, T, J = 512, 512, 2048, 1024
FLOPS = 2 * 2 * K * N * J

F32 = mybir.dt.float32
BF16 = mybir.dt.bfloat16
U32 = mybir.dt.uint32
U16 = mybir.dt.uint16
U8 = mybir.dt.uint8
FP8X4 = mybir.dt.float8_e4m3fn_x4
ALU = mybir.AluOpType
ACT = mybir.ActivationFunctionType

P = 128
PACK = 4
HEADS = 8
HEAD_ROWS = P // HEADS
BANK = 512
N_TILES = N // P
J_BLOCKS = J // P
WIDE = BANK
CHUNK = WIDE // 2
HALF = N // 2
HELD_TILE = 2


def tile_list_max_bias_kernel(tc, xT, wgt, zT, wgt2, wa, wb, b, offs, offs2, out):
    nc = tc.nc
    with ExitStack() as ctx:
        keep = ctx.enter_context(tc.tile_pool(name="keep", bufs=1))
        psum = ctx.enter_context(tc.psum_pool(name="psum", bufs=8))

        def load(name, shape, dtype, src):
            tile = keep.tile(shape, dtype, name=name, tag=name, align_bytes=64)
            nc.sync.dma_start(tile[:], src)
            return tile

        x_rows = xT.rearrange("(p t) s -> p t s", t=PACK)
        z_rows = zT.rearrange("(p t) s -> p t s", t=PACK)
        head_rows = keep.tile([P, P], F32, name="head_rows")
        for s, w in enumerate((wgt, wgt2)):
            rows = w.rearrange("(g r) (c i) -> r g c i", r=HEAD_ROWS, i=P)[0]
            nc.sync.dma_start(head_rows[P // 2 * s : P // 2 * (s + 1), :], rows)
        x_wgt = keep.tile([P, J], F32, name="x_wgt")
        z_wgt = [keep.tile([P, WIDE], F32, name="z_wgt%d" % h, tag="z_wgt%d" % h, align_bytes=64) for h in range(2)]
        nc.sync.dma_start(x_wgt[:, 0:CHUNK], wgt[:, 0:CHUNK])

        x_list = load("x_list", [P, J // HEAD_ROWS], U16, offs)
        x_planes = [load("x_plane%d" % t, [P, T], F32, x_rows[:, t, :]) for t in range(PACK)]
        wa_raw = load("wa_raw", [P, PACK, N], F32, wa.rearrange("(p t) n -> p t n", t=PACK))
        z_list = load("z_list", [P, J // HEAD_ROWS], U16, offs2)
        z_planes = [load("z_plane%d" % t, [P, T], F32, z_rows[:, t, :]) for t in range(PACK - 1)]
        wb_raw = load("wb_raw", [P, PACK, N], F32, wb.rearrange("(p t) n -> p t n", t=PACK))
        z_planes.append(load("z_plane3", [P, T], F32, z_rows[:, PACK - 1, :]))

        ident = keep.tile([P, P], F32, name="ident")
        make_identity(nc, ident[:])
        b_rows = keep.tile([P, P], F32, name="b_rows")
        nc.gpsimd.memset(b_rows[:], 0.0)
        nc.scalar.dma_start(b_rows[0:N_TILES, :], b.rearrange("(m p) -> m p", p=P))

        turned = psum.tile([P, BANK], F32, name="acc")
        nc.tensor.transpose(turned[:, 0:P], head_rows[:], ident[:])
        by_block = turned[:, 0:P].rearrange("i (s g c) -> i s c g", s=2, g=HEADS)

        def spread(s, dst, c0, c1):
            blocks = c1 - c0
            wide = keep.tile([P, blocks, HEADS, HEAD_ROWS], F32, name="wide%d_%d" % (s, c0))
            nc.scalar.copy(wide[:], by_block[:, s, c0:c1, :].unsqueeze(3).to_broadcast([P, blocks, HEADS, HEAD_ROWS]))
            bank = psum.tile([P, BANK], F32, name="acc")
            for c in range(blocks):
                nc.tensor.transpose(
                    bank[:, c * P : (c + 1) * P], wide[:, c, :, :].rearrange("i g r -> i (g r)"), ident[:]
                )
            nc.scalar.copy(dst, bank[:, 0 : blocks * P])

        for j0, j1 in ((CHUNK, CHUNK + BANK), (CHUNK + BANK, J)):
            spread(0, x_wgt[:, j0:j1], j0 // P, j1 // P)
        for h in range(2):
            spread(1, z_wgt[h][:], h * J_BLOCKS // 2, (h + 1) * J_BLOCKS // 2)

        b_turned = psum.tile([P, BANK], F32, name="acc")
        nc.tensor.transpose(b_turned[:, 0:P], b_rows[:], ident[:])
        bias = keep.tile([P, N_TILES], F32, name="bias")
        nc.scalar.copy(bias[:], b_turned[:, 0:N_TILES])

        def gather(dst, plane, offsets, weights, j0, j1):
            picked = plane[:].indirect(offsets[:, j0 // HEAD_ROWS : j1 // HEAD_ROWS])
            nc.vector.tensor_tensor(dst, picked, weights, ALU.mult)

        def weave(copy, dst, src):
            copy(dst.rearrange("p (c i) t -> p c t i", i=4), src.rearrange("p t (c i) -> p c t i", i=4))

        def woven_tile(name, width):
            return keep.tile([P, width, PACK], BF16, name=name, tag=name, align_bytes=64)

        def quantise(name, woven, tag):
            width = woven.shape[1]
            codes = keep.tile([P, width], U32, name=name + "_codes", tag=tag, align_bytes=64)
            scales = keep.tile([P, width], U8, name=name + "_scales", align_bytes=64)
            nc.vector.quantize_mx(
                out=codes[:].bitcast(FP8X4), scales=scales[:], in_=woven.rearrange("p w t -> p (w t)")
            )
            return codes, scales

        def product(w_q, col, a_q):
            acc = psum.tile([P, BANK], F32, name="acc")
            nc.tensor.matmul_mx(
                out=acc[:],
                lhsT=w_q[0][:, col : col + P].bitcast(FP8X4),
                lhsT_scale=w_q[1][:, col : col + P],
                rhs=a_q[0][:].bitcast(FP8X4),
                rhs_scale=a_q[1][:],
                start=True,
                stop=True,
            )
            return acc

        whole = (0, J)
        halves = (0, WIDE, J)
        early = (0, CHUNK, CHUNK + BANK, J)
        late = (0, CHUNK, WIDE, J)
        xg = keep.tile([P, PACK, J], F32, name="xg")
        zg = [keep.tile([P, PACK, WIDE], F32, name="zg%d" % h, tag="zg%d" % h, align_bytes=64) for h in range(2)]
        for t, cuts in enumerate((early, whole, whole, late)):
            for j0, j1 in zip(cuts[:-1], cuts[1:]):
                gather(xg[:, t, j0:j1], x_planes[t], x_list, x_wgt[:, j0:j1], j0, j1)
        for t, cuts in enumerate((halves, halves, halves, late)):
            for j0, j1 in zip(cuts[:-1], cuts[1:]):
                h = j0 // WIDE
                part = slice(j0 - h * WIDE, j1 - h * WIDE)
                gather(zg[h][:, t, part], z_planes[t], z_list, z_wgt[h][:, part], j0, j1)

        x_woven = [woven_tile("x_woven%d" % h, WIDE) for h in range(2)]
        for h in range(2):
            weave(nc.scalar.copy, x_woven[h][:, :, 0:2], xg[:, 0:2, h * WIDE : (h + 1) * WIDE])
        for j0 in (0, CHUNK):
            weave(nc.scalar.copy, x_woven[0][:, j0 : j0 + CHUNK, 2:4], xg[:, 2:4, j0 : j0 + CHUNK])
        wa_woven = woven_tile("wa_woven", N)
        weave(nc.vector.tensor_copy, wa_woven[:, 0:HALF, :], wa_raw[:, :, 0:HALF])
        weave(nc.scalar.copy, wa_woven[:, HALF:N, :], wa_raw[:, :, HALF:N])
        weave(nc.scalar.copy, x_woven[1][:, :, 2:4], xg[:, 2:4, WIDE:J])
        x_q = [quantise("x%d" % h, x_woven[h][:], "x%d_codes" % h) for h in range(2)]
        wa_q = quantise("wa", wa_woven[:], "wa_codes")
        ya = [keep.tile([P, J], F32, name="ya%d" % m) for m in range(N_TILES)]
        for h in range(2):
            for m in range(N_TILES):
                acc = product(wa_q, m * P, x_q[h])
                nc.scalar.activation(ya[m][:, h * WIDE : (h + 1) * WIDE], acc[:], ACT.Identity, bias=bias[:, m : m + 1])

        z_woven = [woven_tile("z_woven%d" % h, WIDE) for h in range(2)]
        wb_woven = woven_tile("wb_woven", N)
        weave(nc.scalar.copy, wb_woven[:], wb_raw[:])
        for j0, j1 in zip(late[:-1], late[1:]):
            h = j0 // WIDE
            part = slice(j0 - h * WIDE, j1 - h * WIDE)
            weave(nc.scalar.copy, z_woven[h][:, part, :], zg[h][:, :, part])
        wb_q = [quantise("wb0", wb_woven[:, 0:HALF, :], "z_wgt0")]
        z_q = [quantise("z0", z_woven[0][:], "z0_codes")]
        wb_q.append(quantise("wb1", wb_woven[:, HALF:N, :], "zg0"))
        z_q.append(quantise("z1", z_woven[1][:], "z1_codes"))

        for h in range(2):
            cols = slice(h * WIDE, (h + 1) * WIDE)
            for m in range(N_TILES):
                name = "res%d_%d" % (h, m)
                tag = "zg1" if (h, m) == (0, HELD_TILE) else name
                res = keep.tile([P, WIDE], F32, name=name, tag=tag, align_bytes=64)
                acc = product(wb_q[m * P // HALF], m * P % HALF, z_q[h])
                nc.vector.scalar_tensor_tensor(
                    out=res[:], in0=acc[:], scalar=bias[:, m : m + 1], in1=ya[m][:, cols], op0=ALU.add, op1=ALU.max
                )
                nc.sync.dma_start(out[m * P : (m + 1) * P, cols], res[:])
